import numpy as np
import ml_dtypes


def mxq(x, axis, fmt="e4m3"):
    dtype, down = {"e4m3": (ml_dtypes.float8_e4m3fn, 7), "e5m2": (ml_dtypes.float8_e5m2, 14)}[fmt]
    v = np.moveaxis(np.asarray(x, np.float32).astype(ml_dtypes.bfloat16).astype(np.float64), axis, -1)
    blocks = v.reshape(v.shape[:-1] + (-1, 32))
    amax = np.abs(blocks).max(-1, keepdims=True)
    byte = np.maximum(np.where(amax > 0, np.frexp(amax)[1] - 1 + 127, 0) - down, 1)
    scale = np.exp2(byte - 127.0)
    codes = (blocks / scale).astype(np.float32).astype(dtype).astype(np.float64)
    return np.moveaxis((codes * scale).reshape(v.shape), -1, axis)


WIDE = False


def mx_kscale(k):
    if not WIDE:
        return np.ones(k)
    levels = np.array([10, -10, 5, -5, 0])
    if k % 512:
        return np.exp2(np.random.permutation(np.resize(levels, k // 32))).repeat(32)
    a = np.empty((k // 512, 16))
    for p in range(k // 512):
        a[p, :8] = np.random.permutation(np.resize(levels, 8))
        for g in range(8):
            far = levels[np.abs(levels - a[p, g]) >= 10]
            a[p, g + 8] = far[np.random.randint(len(far))]
    return np.exp2(a.ravel()).repeat(32)


def f64(x):
    return np.asarray(x).astype(np.float64)


E2M1 = np.array([0.0, 0.5, 1.0, 1.5, 2.0, 3.0, 4.0, 6.0, -0.0, -0.5, -1.0, -1.5, -2.0, -3.0, -4.0, -6.0])


def pack_weight(w, fmt):
    k, n = w.shape
    w = f64(np.asarray(w, np.float32).astype(ml_dtypes.bfloat16)).reshape(k // 32, 32, n)
    amax = np.abs(w).max(1)
    if fmt == "e4m3":
        byte = np.frexp(amax)[1] - 1 + 127 - 7
    else:
        mant, ex = np.frexp(amax / 6.0)
        byte = np.where(mant > 0.5, ex, ex - 1) + 127
    byte = np.clip(np.where(amax > 0, byte, 1), 1, 254)
    scaled = (w * np.exp2(127.0 - byte)[:, None, :]).reshape(k, n).astype(np.float32)
    by_word = np.ascontiguousarray(scaled.reshape(k // 512, 128, 4, n).transpose(0, 1, 3, 2))
    if fmt == "e4m3":
        words = by_word.astype(ml_dtypes.float8_e4m3fn).view(np.uint8)
    else:
        c = by_word.astype(ml_dtypes.float4_e2m1fn).view(np.uint8) & 0xF
        words = (c[..., 0::2] | (c[..., 1::2] << 4)).reshape(k // 512, 128, 2 * n)
    return np.ascontiguousarray(words), np.ascontiguousarray(byte.astype(np.uint8).reshape(k // 512, 16, n))


def unpack_weight(words, scales, fmt):
    g, _, n = scales.shape
    words = np.ascontiguousarray(words).reshape(g, 128, n, -1)
    if fmt == "e4m3":
        vals = words.view(ml_dtypes.float8_e4m3fn).astype(np.float64)
    else:
        nib = np.empty((g, 128, n, 4), np.uint8)
        nib[..., 0::2] = words & 0xF
        nib[..., 1::2] = words >> 4
        vals = E2M1[nib]
    vals = vals * np.repeat(np.exp2(scales.astype(np.float64) - 127.0), 8, axis=1)[..., None]
    return vals.transpose(0, 1, 3, 2).reshape(g * 512, n)


def planes(y):
    n, m = y.shape
    v = y.astype(np.float32).astype(ml_dtypes.bfloat16).astype(np.float64).reshape(n // 32, 32, m)
    top = np.abs(v).max(1)
    byte = np.clip(np.where(top > 0, np.frexp(top)[1] - 1 + 127 - 7, 1), 1, 254)
    codes = (v * np.exp2(127.0 - byte)[:, None, :]).reshape(n, m).astype(np.float32).astype(ml_dtypes.float8_e4m3fn).view(np.uint8)
    words = codes.reshape(n // 512, 128, 4, m).transpose(0, 1, 3, 2)
    return np.ascontiguousarray(words), np.ascontiguousarray(byte.astype(np.uint8).reshape(n // 512, 16, m))


O, K, M, T = 1024, 2048, 512, 1536


def setup_inputs():
    n = np.random.standard_normal
    s = mx_kscale(K)[:, None]
    x = n((K, T)); x[:O] *= 6.0
    w = n((K, M)) / np.sqrt(K) / s; w[:O] /= 2.0
    p_x4 = pack_weight(x[O:] * s[O:], "e2m1")
    p_w4 = pack_weight(w[O:], "e2m1")
    return {
        "x8": (x[:O] * s[:O]).astype(np.float32),
        "w8": (w[:O]).astype(np.float32),
        "x4_words": p_x4[0],
        "x4_scales": p_x4[1],
        "w4_words": p_w4[0],
        "w4_scales": p_w4[1],
    }


def reference(x8, w8, x4_words, x4_scales, w4_words, w4_scales):
    x8_ = mxq(f64(x8), 0, "e4m3")
    w8_ = mxq(f64(w8), 0, "e4m3")
    x4_ = unpack_weight(x4_words, x4_scales, "e2m1")
    w4_ = unpack_weight(w4_words, w4_scales, "e2m1")
    y = w8_.T @ x8_ + w4_.T @ x4_
    out_0 = y
    return (out_0,) + planes(out_0)

@@ -1,0 +1,211 @@
+from contextlib import ExitStack
+
+import concourse.mybir as mybir
+
+O, K4, M, T = 1024, 1024, 512, 1536
+FLOPS = 2 * (O + K4) * M * T
+
+F32 = mybir.dt.float32
+BF16 = mybir.dt.bfloat16
+I32 = mybir.dt.int32
+U32 = mybir.dt.uint32
+U8 = mybir.dt.uint8
+FP8X4 = mybir.dt.float8_e4m3fn_x4
+FP4X4 = mybir.dt.float4_e2m1fn_x4
+
+P = 128
+PACK = 4
+KP = P * PACK
+PASSES = 2
+N = 512
+CHUNKS = T // N
+QUADS = 4
+
+
+def tile_mix_atom_fm_pl_none_kernel(
+    tc, x8, w8, x4_words, x4_scales, w4_words, w4_scales, out_0, out_1, out_2
+):
+    nc = tc.nc
+    with ExitStack() as ctx:
+        sb = ctx.enter_context(tc.tile_pool(name="sb", bufs=1))
+        psum = ctx.enter_context(tc.psum_pool(name="psum", bufs=1))
+        ctx.enter_context(tc.manual_schedule())
+
+        def tile(name, shape, dtype):
+            return sb.tile(shape, dtype, name=name, align_bytes=64)
+
+        w8_raw = [tile("w8_raw%d" % a, [P, PACK, M], F32) for a in range(PASSES)]
+        w8_bf = [tile("w8_bf%d" % a, [P, PACK, P, PACK], BF16) for a in range(PASSES)]
+        w8_codes = [tile("w8_codes%d" % a, [P, M], U32) for a in range(PASSES)]
+        w8_plane = [tile("w8_plane%d" % a, [P, M], U8) for a in range(PASSES)]
+        pieces = [(c, a) for c in range(CHUNKS) for a in range(PASSES)]
+        x8_raw = {k: tile("x8_raw%d_%d" % k, [P, PACK, N], F32) for k in pieces}
+        x8_bf = {k: tile("x8_bf%d_%d" % k, [P, N, PACK], BF16) for k in pieces}
+        x8_codes = {k: tile("x8_codes%d_%d" % k, [P, N], U32) for k in pieces}
+        x8_plane = {k: tile("x8_plane%d_%d" % k, [P, N], U8) for k in pieces}
+        w4_raw = tile("w4_raw", [P, PASSES, 2 * M], U8)
+        w4_dealt = tile("w4_dealt", [P, PASSES, 2 * M], U8)
+        w4_plane_raw = tile("w4_plane_raw", [P, PASSES, M], U8)
+        w4_plane = tile("w4_plane", [P, PASSES, M], U8)
+        x4_codes = tile("x4_codes", [P, PASSES, 2 * T], U8)
+        x4_plane = tile("x4_plane", [P, PASSES, T], U8)
+        y32 = [tile("y32_%d" % c, [P, PACK, N], F32) for c in range(CHUNKS)]
+        y_bf = [tile("y_bf%d" % c, [P, N, PACK], BF16) for c in range(CHUNKS)]
+        y_codes = tile("y_codes", [P, T], U32)
+        y_plane = tile("y_plane", [P, T], U8)
+        acc = {}
+
+        def load_w8(a):
+            rows = w8[a * KP : (a + 1) * KP, :]
+            nc.sync.dma_start(out=w8_raw[a][:], in_=rows.rearrange("(p j) n -> p j n", j=PACK))
+
+        def load_x8(c, a):
+            rows = x8[a * KP : (a + 1) * KP, c * N : (c + 1) * N]
+            nc.sync.dma_start(out=x8_raw[c, a][:], in_=rows.rearrange("(p j) t -> p j t", j=PACK))
+
+        def load_x4(c0, c1):
+            cols = slice(2 * N * c0, 2 * N * c1)
+            nc.sync.dma_start(
+                out=x4_codes[:, :, cols].bitcast(I32),
+                in_=x4_words.rearrange("a p b -> p a b")[:, :, cols].bitcast(I32),
+            )
+
+        def load_plane(plane, scales):
+            for q in range(QUADS):
+                nc.sync.dma_start(
+                    out=plane[32 * q : 32 * q + 4, :, :].bitcast(I32),
+                    in_=scales.rearrange("a q n -> q a n")[4 * q : 4 * q + 4, :, :].bitcast(I32),
+                )
+
+        def interleave(copy, dst, src):
+            copy(
+                out=dst[:].rearrange("p (c i) j -> p c j i", i=4),
+                in_=src[:].rearrange("p j (c i) -> p c j i", i=4),
+            )
+
+        def round_w8(a):
+            nc.scalar.copy(
+                out=w8_bf[a][:].rearrange("p r m j -> p m r j"),
+                in_=w8_raw[a][:].rearrange("p j (m r) -> p m r j", r=PACK),
+            )
+
+        def quantize(codes, plane, src):
+            nc.vector.quantize_mx(out=codes.bitcast(FP8X4), scales=plane, in_=src)
+
+        def quantize_w8(a):
+            quantize(w8_codes[a][:], w8_plane[a][:], w8_bf[a][:].rearrange("p r m j -> p (r m j)"))
+
+        def round_x8(c, a):
+            interleave(nc.vector.tensor_copy, x8_bf[c, a], x8_raw[c, a])
+
+        def quantize_x8(c, a):
+            quantize(x8_codes[c, a][:], x8_plane[c, a][:], x8_bf[c, a][:].rearrange("p t j -> p (t j)"))
+
+        def fp4_passes(c):
+            for r in range(PACK):
+                name = "acc%d_%d" % (c % 2, r)
+                acc[c, r] = psum.tile([P, N], F32, name=name)
+                for a in range(PASSES):
+                    nc.tensor.matmul_mx(
+                        out=acc[c, r][:],
+                        lhsT=w4_dealt[:, a, 2 * P * r : 2 * P * (r + 1)].bitcast(FP4X4),
+                        lhsT_scale=w4_plane[:, a, P * r : P * (r + 1)],
+                        rhs=x4_codes[:, a, 2 * N * c : 2 * N * (c + 1)].bitcast(FP4X4),
+                        rhs_scale=x4_plane[:, a, N * c : N * (c + 1)],
+                        start=(a == 0),
+                        stop=False,
+                    )
+
+        def fp8_passes(c, a):
+            for r in range(PACK):
+                nc.tensor.matmul_mx(
+                    out=acc[c, r][:],
+                    lhsT=w8_codes[a][:, P * r : P * (r + 1)].bitcast(FP8X4),
+                    lhsT_scale=w8_plane[a][:, P * r : P * (r + 1)],
+                    rhs=x8_codes[c, a][:].bitcast(FP8X4),
+                    rhs_scale=x8_plane[c, a][:],
+                    start=False,
+                    stop=(a == PASSES - 1),
+                )
+
+        def drain(c, r, copy):
+            copy(out=y32[c][:, r, :], in_=acc[c, r][:])
+
+        def quantize_y(c):
+            cols = slice(c * N, (c + 1) * N)
+            quantize(y_codes[:, cols], y_plane[:, cols], y_bf[c][:].rearrange("p t j -> p (t j)"))
+
+        def store_y(c):
+            nc.sync.dma_start(
+                out=out_0[:, c * N : (c + 1) * N].rearrange("(p r) t -> p r t", r=PACK), in_=y32[c][:]
+            )
+
+        def store_codes(c0, c1):
+            cols = slice(c0 * N, c1 * N)
+            nc.sync.dma_start(
+                out=out_1.rearrange("a p t i -> p (a t i)").bitcast(I32)[:, cols],
+                in_=y_codes[:, cols].bitcast(I32),
+            )
+
+        nc.vector.memset(w4_plane_raw[:].rearrange("p a n -> p (a n)").bitcast(I32), 0)
+        nc.vector.memset(x4_plane[:].rearrange("p a n -> p (a n)").bitcast(I32), 0)
+
+        load_w8(0)
+        load_plane(w4_plane_raw, w4_scales)
+        nc.sync.dma_start(
+            out=w4_raw[:].bitcast(I32), in_=w4_words.rearrange("a p b -> p a b").bitcast(I32)
+        )
+        load_x4(0, 2)
+        load_w8(1)
+        load_plane(x4_plane, x4_scales)
+        for c in range(CHUNKS):
+            if c == CHUNKS - 1:
+                load_x4(2, 3)
+            for a in range(PASSES):
+                load_x8(c, a)
+
+        round_w8(0)
+        round_w8(1)
+        for a in range(PASSES):
+            nc.vector.tensor_copy(
+                out=w4_dealt[:, a, :].rearrange("p (r m b) -> p r m b", r=PACK, b=2),
+                in_=w4_raw[:, a, :].rearrange("p (m r b) -> p r m b", r=PACK, b=2),
+            )
+        nc.vector.tensor_copy(
+            out=w4_plane[:].rearrange("p a (r m) -> p a r m", r=PACK),
+            in_=w4_plane_raw[:].rearrange("p a (m r) -> p a r m", r=PACK),
+        )
+        quantize_w8(0)
+
+        last = CHUNKS - 1
+        for c in range(CHUNKS):
+            fp4_passes(c)
+            round_x8(c, 0)
+            if c == 0:
+                quantize_w8(1)
+            quantize_x8(c, 0)
+            fp8_passes(c, 0)
+            if c == last:
+                quantize_y(0)
+            round_x8(c, 1)
+            quantize_x8(c, 1)
+            fp8_passes(c, 1)
+            if c < last:
+                for r in range(PACK):
+                    drain(c, r, nc.scalar.copy)
+                interleave(nc.scalar.copy, y_bf[c], y32[c])
+        store_y(0)
+        store_y(1)
+        quantize_y(1)
+        store_codes(0, 2)
+        for r in range(PACK):
+            drain(last, r, nc.scalar.copy if r % 2 == 0 else nc.vector.tensor_copy)
+        store_y(last)
+        interleave(nc.vector.tensor_copy, y_bf[last], y32[last])
+        quantize_y(last)
+        store_codes(last, CHUNKS)
+        for q in range(QUADS):
+            nc.scalar.dma_start(
+                out=out_2[0, 4 * q : 4 * q + 4, :].bitcast(I32),
+                in_=y_plane[32 * q : 32 * q + 4, :].bitcast(I32),
+            )

@@ -20,6 +20,7 @@ PASSES = 2
 N = 512
 CHUNKS = T // N
 QUADS = 4
+SPLIT = 320
 
 
 def tile_mix_atom_fm_pl_none_kernel(
@@ -47,7 +48,9 @@ def tile_mix_atom_fm_pl_none_kernel(
         w4_dealt = tile("w4_dealt", [P, PASSES, 2 * M], U8)
         w4_plane_raw = tile("w4_plane_raw", [P, PASSES, M], U8)
         w4_plane = tile("w4_plane", [P, PASSES, M], U8)
-        x4_codes = tile("x4_codes", [P, PASSES, 2 * T], U8)
+        x4_early = tile("x4_early", [P, PASSES, 4 * N], U8)
+        x4_late = tile("x4_late", [P, PASSES, 2 * N], U8)
+        x4_codes = [x4_early[:, :, : 2 * N], x4_early[:, :, 2 * N :], x4_late[:]]
         x4_plane = tile("x4_plane", [P, PASSES, T], U8)
         y32 = [tile("y32_%d" % c, [P, PACK, N], F32) for c in range(CHUNKS)]
         y_bf = [tile("y_bf%d" % c, [P, N, PACK], BF16) for c in range(CHUNKS)]
@@ -63,10 +66,10 @@ def tile_mix_atom_fm_pl_none_kernel(
             rows = x8[a * KP : (a + 1) * KP, c * N : (c + 1) * N]
             nc.sync.dma_start(out=x8_raw[c, a][:], in_=rows.rearrange("(p j) t -> p j t", j=PACK))
 
-        def load_x4(c0, c1):
+        def load_x4(dst, c0, c1):
             cols = slice(2 * N * c0, 2 * N * c1)
             nc.sync.dma_start(
-                out=x4_codes[:, :, cols].bitcast(I32),
+                out=dst[:].bitcast(I32),
                 in_=x4_words.rearrange("a p b -> p a b")[:, :, cols].bitcast(I32),
             )
 
@@ -79,8 +82,8 @@ def tile_mix_atom_fm_pl_none_kernel(
 
         def interleave(copy, dst, src):
             copy(
-                out=dst[:].rearrange("p (c i) j -> p c j i", i=4),
-                in_=src[:].rearrange("p j (c i) -> p c j i", i=4),
+                out=dst.rearrange("p (c i) j -> p c j i", i=4),
+                in_=src.rearrange("p j (c i) -> p c j i", i=4),
             )
 
         def round_w8(a):
@@ -96,7 +99,7 @@ def tile_mix_atom_fm_pl_none_kernel(
             quantize(w8_codes[a][:], w8_plane[a][:], w8_bf[a][:].rearrange("p r m j -> p (r m j)"))
 
         def round_x8(c, a):
-            interleave(nc.vector.tensor_copy, x8_bf[c, a], x8_raw[c, a])
+            interleave(nc.vector.tensor_copy, x8_bf[c, a][:], x8_raw[c, a][:])
 
         def quantize_x8(c, a):
             quantize(x8_codes[c, a][:], x8_plane[c, a][:], x8_bf[c, a][:].rearrange("p t j -> p (t j)"))
@@ -110,7 +113,7 @@ def tile_mix_atom_fm_pl_none_kernel(
                         out=acc[c, r][:],
                         lhsT=w4_dealt[:, a, 2 * P * r : 2 * P * (r + 1)].bitcast(FP4X4),
                         lhsT_scale=w4_plane[:, a, P * r : P * (r + 1)],
-                        rhs=x4_codes[:, a, 2 * N * c : 2 * N * (c + 1)].bitcast(FP4X4),
+                        rhs=x4_codes[c][:, a, :].bitcast(FP4X4),
                         rhs_scale=x4_plane[:, a, N * c : N * (c + 1)],
                         start=(a == 0),
                         stop=False,
@@ -155,12 +158,12 @@ def tile_mix_atom_fm_pl_none_kernel(
         nc.sync.dma_start(
             out=w4_raw[:].bitcast(I32), in_=w4_words.rearrange("a p b -> p a b").bitcast(I32)
         )
-        load_x4(0, 2)
+        load_x4(x4_early, 0, 2)
         load_w8(1)
         load_plane(x4_plane, x4_scales)
         for c in range(CHUNKS):
             if c == CHUNKS - 1:
-                load_x4(2, 3)
+                load_x4(x4_late, 2, 3)
             for a in range(PASSES):
                 load_x8(c, a)
 
@@ -193,7 +196,7 @@ def tile_mix_atom_fm_pl_none_kernel(
             if c < last:
                 for r in range(PACK):
                     drain(c, r, nc.scalar.copy)
-                interleave(nc.scalar.copy, y_bf[c], y32[c])
+                interleave(nc.scalar.copy, y_bf[c][:], y32[c][:])
         store_y(0)
         store_y(1)
         quantize_y(1)
@@ -201,7 +204,8 @@ def tile_mix_atom_fm_pl_none_kernel(
         for r in range(PACK):
             drain(last, r, nc.scalar.copy if r % 2 == 0 else nc.vector.tensor_copy)
         store_y(last)
-        interleave(nc.vector.tensor_copy, y_bf[last], y32[last])
+        interleave(nc.vector.tensor_copy, y_bf[last][:, :SPLIT, :], y32[last][:, :, :SPLIT])
+        interleave(nc.scalar.copy, y_bf[last][:, SPLIT:, :], y32[last][:, :, SPLIT:])
         quantize_y(last)
         store_codes(last, CHUNKS)
         for q in range(QUADS):

@@ -18,8 +18,8 @@ PACK = 4
 KP = P * PACK
 PASSES = 2
 N = 512
+H = N // 2
 CHUNKS = T // N
-QUADS = 4
 SPLIT = 320
 
 
@@ -39,18 +39,16 @@ def tile_mix_atom_fm_pl_none_kernel(
         w8_bf = [tile("w8_bf%d" % a, [P, PACK, P, PACK], BF16) for a in range(PASSES)]
         w8_codes = [tile("w8_codes%d" % a, [P, M], U32) for a in range(PASSES)]
         w8_plane = [tile("w8_plane%d" % a, [P, M], U8) for a in range(PASSES)]
-        pieces = [(c, a) for c in range(CHUNKS) for a in range(PASSES)]
-        x8_raw = {k: tile("x8_raw%d_%d" % k, [P, PACK, N], F32) for k in pieces}
-        x8_bf = {k: tile("x8_bf%d_%d" % k, [P, N, PACK], BF16) for k in pieces}
-        x8_codes = {k: tile("x8_codes%d_%d" % k, [P, N], U32) for k in pieces}
-        x8_plane = {k: tile("x8_plane%d_%d" % k, [P, N], U8) for k in pieces}
+        pieces = [(0, t0, N) for t0 in range(0, T, N)] + [(1, 0, N), (1, N, N), (1, 2 * N, H), (1, 2 * N + H, H)]
+        x8_raw = {k: tile("x8_raw%d_%d" % k[:2], [P, PACK, k[2]], F32) for k in pieces}
+        x8_bf = {k: tile("x8_bf%d_%d" % k[:2], [P, k[2], PACK], BF16) for k in pieces}
+        x8_codes = {k: tile("x8_codes%d_%d" % k[:2], [P, k[2]], U32) for k in pieces}
+        x8_plane = {k: tile("x8_plane%d_%d" % k[:2], [P, k[2]], U8) for k in pieces}
         w4_raw = tile("w4_raw", [P, PASSES, 2 * M], U8)
         w4_dealt = tile("w4_dealt", [P, PASSES, 2 * M], U8)
         w4_plane_raw = tile("w4_plane_raw", [P, PASSES, M], U8)
         w4_plane = tile("w4_plane", [P, PASSES, M], U8)
-        x4_early = tile("x4_early", [P, PASSES, 4 * N], U8)
-        x4_late = tile("x4_late", [P, PASSES, 2 * N], U8)
-        x4_codes = [x4_early[:, :, : 2 * N], x4_early[:, :, 2 * N :], x4_late[:]]
+        x4_codes = tile("x4_codes", [P, PASSES, 2 * T], U8)
         x4_plane = tile("x4_plane", [P, PASSES, T], U8)
         y32 = [tile("y32_%d" % c, [P, PACK, N], F32) for c in range(CHUNKS)]
         y_bf = [tile("y_bf%d" % c, [P, N, PACK], BF16) for c in range(CHUNKS)]
@@ -62,23 +60,18 @@ def tile_mix_atom_fm_pl_none_kernel(
             rows = w8[a * KP : (a + 1) * KP, :]
             nc.sync.dma_start(out=w8_raw[a][:], in_=rows.rearrange("(p j) n -> p j n", j=PACK))
 
-        def load_x8(c, a):
-            rows = x8[a * KP : (a + 1) * KP, c * N : (c + 1) * N]
-            nc.sync.dma_start(out=x8_raw[c, a][:], in_=rows.rearrange("(p j) t -> p j t", j=PACK))
+        def load_x8(k):
+            a, t0, width = k
+            rows = x8[a * KP : (a + 1) * KP, t0 : t0 + width]
+            nc.sync.dma_start(out=x8_raw[k][:], in_=rows.rearrange("(p j) t -> p j t", j=PACK))
 
-        def load_x4(dst, c0, c1):
-            cols = slice(2 * N * c0, 2 * N * c1)
-            nc.sync.dma_start(
-                out=dst[:].bitcast(I32),
-                in_=x4_words.rearrange("a p b -> p a b")[:, :, cols].bitcast(I32),
-            )
+        def load_words(dst, words):
+            nc.sync.dma_start(out=dst[:].bitcast(I32), in_=words.rearrange("a p b -> p a b").bitcast(I32))
 
         def load_plane(plane, scales):
-            for q in range(QUADS):
-                nc.sync.dma_start(
-                    out=plane[32 * q : 32 * q + 4, :, :].bitcast(I32),
-                    in_=scales.rearrange("a q n -> q a n")[4 * q : 4 * q + 4, :, :].bitcast(I32),
-                )
+            rows = scales.rearrange("a (q s) n -> s q a n", s=4)
+            for s in range(4):
+                nc.sync.dma_start(out=plane[s:P:32, :, :].bitcast(I32), in_=rows[s].bitcast(I32))
 
         def interleave(copy, dst, src):
             copy(
@@ -98,14 +91,14 @@ def tile_mix_atom_fm_pl_none_kernel(
         def quantize_w8(a):
             quantize(w8_codes[a][:], w8_plane[a][:], w8_bf[a][:].rearrange("p r m j -> p (r m j)"))
 
-        def round_x8(c, a):
-            interleave(nc.vector.tensor_copy, x8_bf[c, a][:], x8_raw[c, a][:])
+        def round_x8(k):
+            interleave(nc.vector.tensor_copy, x8_bf[k][:], x8_raw[k][:])
 
-        def quantize_x8(c, a):
-            quantize(x8_codes[c, a][:], x8_plane[c, a][:], x8_bf[c, a][:].rearrange("p t j -> p (t j)"))
+        def quantize_x8(k):
+            quantize(x8_codes[k][:], x8_plane[k][:], x8_bf[k][:].rearrange("p t j -> p (t j)"))
 
-        def fp4_passes(c):
-            for r in range(PACK):
+        def fp4_passes(c, tiles=range(PACK)):
+            for r in tiles:
                 name = "acc%d_%d" % (c % 2, r)
                 acc[c, r] = psum.tile([P, N], F32, name=name)
                 for a in range(PASSES):
@@ -113,22 +106,24 @@ def tile_mix_atom_fm_pl_none_kernel(
                         out=acc[c, r][:],
                         lhsT=w4_dealt[:, a, 2 * P * r : 2 * P * (r + 1)].bitcast(FP4X4),
                         lhsT_scale=w4_plane[:, a, P * r : P * (r + 1)],
-                        rhs=x4_codes[c][:, a, :].bitcast(FP4X4),
+                        rhs=x4_codes[:, a, 2 * N * c : 2 * N * (c + 1)].bitcast(FP4X4),
                         rhs_scale=x4_plane[:, a, N * c : N * (c + 1)],
                         start=(a == 0),
                         stop=False,
                     )
 
-        def fp8_passes(c, a):
+        def fp8_passes(k):
+            a, t0, width = k
+            c, col = divmod(t0, N)
             for r in range(PACK):
                 nc.tensor.matmul_mx(
-                    out=acc[c, r][:],
+                    out=acc[c, r][:, col : col + width],
                     lhsT=w8_codes[a][:, P * r : P * (r + 1)].bitcast(FP8X4),
                     lhsT_scale=w8_plane[a][:, P * r : P * (r + 1)],
-                    rhs=x8_codes[c, a][:].bitcast(FP8X4),
-                    rhs_scale=x8_plane[c, a][:],
+                    rhs=x8_codes[k][:].bitcast(FP8X4),
+                    rhs_scale=x8_plane[k][:],
                     start=False,
-                    stop=(a == PASSES - 1),
+                    stop=(a == PASSES - 1 and col + width == N),
                 )
 
         def drain(c, r, copy):
@@ -138,10 +133,9 @@ def tile_mix_atom_fm_pl_none_kernel(
             cols = slice(c * N, (c + 1) * N)
             quantize(y_codes[:, cols], y_plane[:, cols], y_bf[c][:].rearrange("p t j -> p (t j)"))
 
-        def store_y(c):
-            nc.sync.dma_start(
-                out=out_0[:, c * N : (c + 1) * N].rearrange("(p r) t -> p r t", r=PACK), in_=y32[c][:]
-            )
+        def store_y(c, r0, r1):
+            rows = out_0.rearrange("(p r) t -> p r t", r=PACK)
+            nc.sync.dma_start(out=rows[:, r0:r1, c * N : (c + 1) * N], in_=y32[c][:, r0:r1, :])
 
         def store_codes(c0, c1):
             cols = slice(c0 * N, c1 * N)
@@ -153,63 +147,80 @@ def tile_mix_atom_fm_pl_none_kernel(
         nc.vector.memset(w4_plane_raw[:].rearrange("p a n -> p (a n)").bitcast(I32), 0)
         nc.vector.memset(x4_plane[:].rearrange("p a n -> p (a n)").bitcast(I32), 0)
 
-        load_w8(0)
+        load_words(x4_codes, x4_words)
         load_plane(w4_plane_raw, w4_scales)
-        nc.sync.dma_start(
-            out=w4_raw[:].bitcast(I32), in_=w4_words.rearrange("a p b -> p a b").bitcast(I32)
-        )
-        load_x4(x4_early, 0, 2)
-        load_w8(1)
+        load_words(w4_raw, w4_words)
+        load_w8(0)
         load_plane(x4_plane, x4_scales)
-        for c in range(CHUNKS):
-            if c == CHUNKS - 1:
-                load_x4(x4_late, 2, 3)
-            for a in range(PASSES):
-                load_x8(c, a)
+        load_w8(1)
+        for k in sorted(pieces, key=lambda k: (k[1] // N, k[0], k[1])):
+            load_x8(k)
 
         round_w8(0)
         round_w8(1)
+        nc.vector.tensor_copy(
+            out=w4_plane[:].rearrange("p a (r m) -> p a r m", r=PACK),
+            in_=w4_plane_raw[:].rearrange("p a (m r) -> p a r m", r=PACK),
+        )
         for a in range(PASSES):
             nc.vector.tensor_copy(
                 out=w4_dealt[:, a, :].rearrange("p (r m b) -> p r m b", r=PACK, b=2),
                 in_=w4_raw[:, a, :].rearrange("p (m r b) -> p r m b", r=PACK, b=2),
             )
-        nc.vector.tensor_copy(
-            out=w4_plane[:].rearrange("p a (r m) -> p a r m", r=PACK),
-            in_=w4_plane_raw[:].rearrange("p a (m r) -> p a r m", r=PACK),
-        )
         quantize_w8(0)
 
+        def prepare_x8(k):
+            round_x8(k)
+            quantize_x8(k)
+
+        def finish_on_scalar(c):
+            for r in range(PACK):
+                drain(c, r, nc.scalar.copy)
+            interleave(nc.scalar.copy, y_bf[c][:], y32[c][:])
+
+        fp4_passes(0)
+        fp4_passes(1)
+        round_x8((0, 0, N))
+        quantize_w8(1)
+        quantize_x8((0, 0, N))
+        fp8_passes((0, 0, N))
+        prepare_x8((1, 0, N))
+        fp8_passes((1, 0, N))
+        finish_on_scalar(0)
+
+        prepare_x8((0, N, N))
+        fp8_passes((0, N, N))
+        fp4_passes(2, (0, 1))
+        prepare_x8((1, N, N))
+        fp8_passes((1, N, N))
+        finish_on_scalar(1)
+
         last = CHUNKS - 1
-        for c in range(CHUNKS):
-            fp4_passes(c)
-            round_x8(c, 0)
-            if c == 0:
-                quantize_w8(1)
-            quantize_x8(c, 0)
-            fp8_passes(c, 0)
-            if c == last:
-                quantize_y(0)
-            round_x8(c, 1)
-            quantize_x8(c, 1)
-            fp8_passes(c, 1)
-            if c < last:
-                for r in range(PACK):
-                    drain(c, r, nc.scalar.copy)
-                interleave(nc.scalar.copy, y_bf[c][:], y32[c][:])
-        store_y(0)
-        store_y(1)
-        quantize_y(1)
-        store_codes(0, 2)
+        halves = pieces[-2:]
+        fp4_passes(last, (2, 3))
+        prepare_x8((0, 2 * N, N))
+        fp8_passes((0, 2 * N, N))
+        for k in halves:
+            round_x8(k)
+        for k in halves:
+            quantize_x8(k)
+            fp8_passes(k)
+
+        store_y(0, 0, 4)
+        store_y(1, 0, 2)
+        store_y(1, 2, 4)
+        quantize_y(0)
+        store_codes(0, 1)
         for r in range(PACK):
-            drain(last, r, nc.scalar.copy if r % 2 == 0 else nc.vector.tensor_copy)
-        store_y(last)
+            drain(last, r, nc.vector.tensor_copy if r < 2 else nc.scalar.copy)
+        store_y(last, 0, 2)
+        store_y(last, 2, 4)
+        quantize_y(1)
+        store_codes(1, 2)
         interleave(nc.vector.tensor_copy, y_bf[last][:, :SPLIT, :], y32[last][:, :, :SPLIT])
         interleave(nc.scalar.copy, y_bf[last][:, SPLIT:, :], y32[last][:, :, SPLIT:])
         quantize_y(last)
         store_codes(last, CHUNKS)
-        for q in range(QUADS):
-            nc.scalar.dma_start(
-                out=out_2[0, 4 * q : 4 * q + 4, :].bitcast(I32),
-                in_=y_plane[32 * q : 32 * q + 4, :].bitcast(I32),
-            )
+        scale_rows = out_2.rearrange("a (q s) t -> s q (a t)", s=4)
+        for s in range(4):
+            nc.scalar.dma_start(out=scale_rows[s].bitcast(I32), in_=y_plane[s:P:32, :].bitcast(I32))

@@ -33,7 +33,7 @@ def tile_mix_atom_fm_pl_none_kernel(
         ctx.enter_context(tc.manual_schedule())
 
         def tile(name, shape, dtype):
-            return sb.tile(shape, dtype, name=name, align_bytes=64)
+            return sb.tile(shape, dtype, name=name, align_bytes=256)
 
         w8_raw = [tile("w8_raw%d" % a, [P, PACK, M], F32) for a in range(PASSES)]
         w8_bf = [tile("w8_bf%d" % a, [P, PACK, P, PACK], BF16) for a in range(PASSES)]

@@ -48,7 +48,8 @@ def tile_mix_atom_fm_pl_none_kernel(
         w4_dealt = tile("w4_dealt", [P, PASSES, 2 * M], U8)
         w4_plane_raw = tile("w4_plane_raw", [P, PASSES, M], U8)
         w4_plane = tile("w4_plane", [P, PASSES, M], U8)
-        x4_codes = tile("x4_codes", [P, PASSES, 2 * T], U8)
+        x4_early = tile("x4_early", [P, PASSES, 4 * N], U8)
+        x4_late = tile("x4_late", [P, PASSES, 2 * N], U8)
         x4_plane = tile("x4_plane", [P, PASSES, T], U8)
         y32 = [tile("y32_%d" % c, [P, PACK, N], F32) for c in range(CHUNKS)]
         y_bf = [tile("y_bf%d" % c, [P, N, PACK], BF16) for c in range(CHUNKS)]
@@ -79,10 +80,10 @@ def tile_mix_atom_fm_pl_none_kernel(
                 in_=src.rearrange("p j (c i) -> p c j i", i=4),
             )
 
-        def round_w8(a):
-            nc.scalar.copy(
-                out=w8_bf[a][:].rearrange("p r m j -> p m r j"),
-                in_=w8_raw[a][:].rearrange("p j (m r) -> p m r j", r=PACK),
+        def round_w8(a, copy, m0, m1):
+            copy(
+                out=w8_bf[a][:, :, m0:m1, :].rearrange("p r m j -> p m r j"),
+                in_=w8_raw[a][:, :, PACK * m0 : PACK * m1].rearrange("p j (m r) -> p m r j", r=PACK),
             )
 
         def quantize(codes, plane, src):
@@ -106,7 +107,7 @@ def tile_mix_atom_fm_pl_none_kernel(
                         out=acc[c, r][:],
                         lhsT=w4_dealt[:, a, 2 * P * r : 2 * P * (r + 1)].bitcast(FP4X4),
                         lhsT_scale=w4_plane[:, a, P * r : P * (r + 1)],
-                        rhs=x4_codes[:, a, 2 * N * c : 2 * N * (c + 1)].bitcast(FP4X4),
+                        rhs=(x4_late[:, a, :] if c == CHUNKS - 1 else x4_early[:, a, 2 * N * c : 2 * N * (c + 1)]).bitcast(FP4X4),
                         rhs_scale=x4_plane[:, a, N * c : N * (c + 1)],
                         start=(a == 0),
                         stop=False,
@@ -129,9 +130,12 @@ def tile_mix_atom_fm_pl_none_kernel(
         def drain(c, r, copy):
             copy(out=y32[c][:, r, :], in_=acc[c, r][:])
 
-        def quantize_y(c):
-            cols = slice(c * N, (c + 1) * N)
-            quantize(y_codes[:, cols], y_plane[:, cols], y_bf[c][:].rearrange("p t j -> p (t j)"))
+        def round_y(c, copy, lo, hi):
+            interleave(copy, y_bf[c][:, lo:hi, :], y32[c][:, :, lo:hi])
+
+        def quantize_y(c, lo=0, hi=N):
+            cols = slice(c * N + lo, c * N + hi)
+            quantize(y_codes[:, cols], y_plane[:, cols], y_bf[c][:, lo:hi, :].rearrange("p t j -> p (t j)"))
 
         def store_y(c, r0, r1):
             rows = out_0.rearrange("(p r) t -> p r t", r=PACK)
@@ -147,17 +151,19 @@ def tile_mix_atom_fm_pl_none_kernel(
         nc.vector.memset(w4_plane_raw[:].rearrange("p a n -> p (a n)").bitcast(I32), 0)
         nc.vector.memset(x4_plane[:].rearrange("p a n -> p (a n)").bitcast(I32), 0)
 
-        load_words(x4_codes, x4_words)
+        load_words(x4_early, x4_words[:, :, : 4 * N])
         load_plane(w4_plane_raw, w4_scales)
         load_words(w4_raw, w4_words)
         load_w8(0)
         load_plane(x4_plane, x4_scales)
         load_w8(1)
         for k in sorted(pieces, key=lambda k: (k[1] // N, k[0], k[1])):
+            if k == (0, 2 * N, N):
+                load_words(x4_late, x4_words[:, :, 4 * N :])
             load_x8(k)
 
-        round_w8(0)
-        round_w8(1)
+        round_w8(0, nc.scalar.copy, 0, P)
+        round_w8(1, nc.scalar.copy, 0, P // 2)
         nc.vector.tensor_copy(
             out=w4_plane[:].rearrange("p a (r m) -> p a r m", r=PACK),
             in_=w4_plane_raw[:].rearrange("p a (m r) -> p a r m", r=PACK),
@@ -167,36 +173,44 @@ def tile_mix_atom_fm_pl_none_kernel(
                 out=w4_dealt[:, a, :].rearrange("p (r m b) -> p r m b", r=PACK, b=2),
                 in_=w4_raw[:, a, :].rearrange("p (m r b) -> p r m b", r=PACK, b=2),
             )
+        vcopy, scopy = nc.vector.tensor_copy, nc.scalar.copy
         quantize_w8(0)
+        round_w8(1, vcopy, P // 2, P)
+        quantize_w8(1)
 
         def prepare_x8(k):
             round_x8(k)
             quantize_x8(k)
 
-        def finish_on_scalar(c):
-            for r in range(PACK):
-                drain(c, r, nc.scalar.copy)
-            interleave(nc.scalar.copy, y_bf[c][:], y32[c][:])
+        last = CHUNKS - 1
+        halves = pieces[-2:]
 
         fp4_passes(0)
         fp4_passes(1)
-        round_x8((0, 0, N))
-        quantize_w8(1)
-        quantize_x8((0, 0, N))
+        prepare_x8((0, 0, N))
         fp8_passes((0, 0, N))
-        prepare_x8((1, 0, N))
-        fp8_passes((1, 0, N))
-        finish_on_scalar(0)
+        k = (1, 0, N)
+        interleave(scopy, x8_bf[k][:, SPLIT:, :], x8_raw[k][:, :, SPLIT:])
+        interleave(vcopy, x8_bf[k][:, :SPLIT, :], x8_raw[k][:, :, :SPLIT])
+        quantize_x8(k)
+        fp8_passes(k)
+        for r in range(PACK):
+            drain(0, r, scopy)
+        round_y(0, scopy, 0, H)
+        round_y(0, scopy, H, N)
+        store_y(0, 0, 4)
 
         prepare_x8((0, N, N))
         fp8_passes((0, N, N))
-        fp4_passes(2, (0, 1))
+        fp4_passes(last, (0, 1))
         prepare_x8((1, N, N))
         fp8_passes((1, N, N))
-        finish_on_scalar(1)
+        for r in range(PACK):
+            drain(1, r, scopy)
+        quantize_y(0, 0, H)
+        store_y(1, 0, 4)
+        round_y(1, scopy, 0, N)
 
-        last = CHUNKS - 1
-        halves = pieces[-2:]
         fp4_passes(last, (2, 3))
         prepare_x8((0, 2 * N, N))
         fp8_passes((0, 2 * N, N))
@@ -205,20 +219,16 @@ def tile_mix_atom_fm_pl_none_kernel(
         for k in halves:
             quantize_x8(k)
             fp8_passes(k)
-
-        store_y(0, 0, 4)
-        store_y(1, 0, 2)
-        store_y(1, 2, 4)
-        quantize_y(0)
+        quantize_y(0, H, N)
         store_codes(0, 1)
         for r in range(PACK):
-            drain(last, r, nc.vector.tensor_copy if r < 2 else nc.scalar.copy)
+            drain(last, r, scopy if r % 2 else vcopy)
         store_y(last, 0, 2)
         store_y(last, 2, 4)
         quantize_y(1)
         store_codes(1, 2)
-        interleave(nc.vector.tensor_copy, y_bf[last][:, :SPLIT, :], y32[last][:, :, :SPLIT])
-        interleave(nc.scalar.copy, y_bf[last][:, SPLIT:, :], y32[last][:, :, SPLIT:])
+        round_y(last, scopy, H, N)
+        round_y(last, vcopy, 0, H)
         quantize_y(last)
         store_codes(last, CHUNKS)
         scale_rows = out_2.rearrange("a (q s) t -> s q (a t)", s=4)

@@ -113,10 +113,10 @@ def tile_mix_atom_fm_pl_none_kernel(
                         stop=False,
                     )
 
-        def fp8_passes(k):
+        def fp8_passes(k, tiles=range(PACK)):
             a, t0, width = k
             c, col = divmod(t0, N)
-            for r in range(PACK):
+            for r in tiles:
                 nc.tensor.matmul_mx(
                     out=acc[c, r][:, col : col + width],
                     lhsT=w8_codes[a][:, P * r : P * (r + 1)].bitcast(FP8X4),
@@ -209,27 +209,32 @@ def tile_mix_atom_fm_pl_none_kernel(
             drain(1, r, scopy)
         quantize_y(0, 0, H)
         store_y(1, 0, 4)
-        round_y(1, scopy, 0, N)
+        round_y(1, scopy, 0, 384)
 
         fp4_passes(last, (2, 3))
-        prepare_x8((0, 2 * N, N))
+        round_x8((0, 2 * N, N))
+        quantize_y(0, H, N)
+        store_codes(0, 1)
+        quantize_x8((0, 2 * N, N))
         fp8_passes((0, 2 * N, N))
         for k in halves:
             round_x8(k)
         for k in halves:
             quantize_x8(k)
-            fp8_passes(k)
-        quantize_y(0, H, N)
-        store_codes(0, 1)
+        for u in range(2):
+            for k in halves:
+                fp8_passes(k, (2 * u, 2 * u + 1))
+        round_y(1, vcopy, 384, N)
         for r in range(PACK):
             drain(last, r, scopy if r % 2 else vcopy)
         store_y(last, 0, 2)
         store_y(last, 2, 4)
+        round_y(last, scopy, 0, H)
         quantize_y(1)
         store_codes(1, 2)
-        round_y(last, scopy, H, N)
-        round_y(last, vcopy, 0, H)
-        quantize_y(last)
+        round_y(last, vcopy, H, N)
+        quantize_y(last, 0, H)
+        quantize_y(last, H, N)
         store_codes(last, CHUNKS)
         scale_rows = out_2.rearrange("a (q s) t -> s q (a t)", s=4)
         for s in range(4):

@@ -141,8 +141,8 @@ def tile_mix_atom_fm_pl_none_kernel(
             rows = out_0.rearrange("(p r) t -> p r t", r=PACK)
             nc.sync.dma_start(out=rows[:, r0:r1, c * N : (c + 1) * N], in_=y32[c][:, r0:r1, :])
 
-        def store_codes(c0, c1):
-            cols = slice(c0 * N, c1 * N)
+        def store_codes(t0, t1):
+            cols = slice(t0, t1)
             nc.sync.dma_start(
                 out=out_1.rearrange("a p t i -> p (a t i)").bitcast(I32)[:, cols],
                 in_=y_codes[:, cols].bitcast(I32),
@@ -209,12 +209,13 @@ def tile_mix_atom_fm_pl_none_kernel(
             drain(1, r, scopy)
         quantize_y(0, 0, H)
         store_y(1, 0, 4)
-        round_y(1, scopy, 0, 384)
+        round_y(1, scopy, 0, H)
+        round_y(1, scopy, H, 384)
 
         fp4_passes(last, (2, 3))
         round_x8((0, 2 * N, N))
         quantize_y(0, H, N)
-        store_codes(0, 1)
+        store_codes(0, N)
         quantize_x8((0, 2 * N, N))
         fp8_passes((0, 2 * N, N))
         for k in halves:
@@ -225,17 +226,18 @@ def tile_mix_atom_fm_pl_none_kernel(
             for k in halves:
                 fp8_passes(k, (2 * u, 2 * u + 1))
         round_y(1, vcopy, 384, N)
+        quantize_y(1, 0, H)
         for r in range(PACK):
             drain(last, r, scopy if r % 2 else vcopy)
         store_y(last, 0, 2)
         store_y(last, 2, 4)
-        round_y(last, scopy, 0, H)
-        quantize_y(1)
-        store_codes(1, 2)
-        round_y(last, vcopy, H, N)
+        round_y(last, scopy, H, N)
+        round_y(last, vcopy, 0, H)
+        quantize_y(1, H, N)
         quantize_y(last, 0, H)
+        store_codes(N, T - H)
         quantize_y(last, H, N)
-        store_codes(last, CHUNKS)
+        store_codes(T - H, T)
         scale_rows = out_2.rearrange("a (q s) t -> s q (a t)", s=4)
         for s in range(4):
             nc.scalar.dma_start(out=scale_rows[s].bitcast(I32), in_=y_plane[s:P:32, :].bitcast(I32))

@@ -35,11 +35,11 @@ def tile_mix_atom_fm_pl_none_kernel(
         def tile(name, shape, dtype):
             return sb.tile(shape, dtype, name=name, align_bytes=256)
 
-        w8_raw = [tile("w8_raw%d" % a, [P, PACK, M], F32) for a in range(PASSES)]
+        w8_raw = tile("w8_raw", [P, PASSES, PACK * M], F32)
         w8_bf = [tile("w8_bf%d" % a, [P, PACK, P, PACK], BF16) for a in range(PASSES)]
         w8_codes = [tile("w8_codes%d" % a, [P, M], U32) for a in range(PASSES)]
         w8_plane = [tile("w8_plane%d" % a, [P, M], U8) for a in range(PASSES)]
-        pieces = [(0, t0, N) for t0 in range(0, T, N)] + [(1, 0, N), (1, N, N), (1, 2 * N, H), (1, 2 * N + H, H)]
+        pieces = [(a, t0, N) for t0 in range(0, T, N) for a in range(PASSES)]
         x8_raw = {k: tile("x8_raw%d_%d" % k[:2], [P, PACK, k[2]], F32) for k in pieces}
         x8_bf = {k: tile("x8_bf%d_%d" % k[:2], [P, k[2], PACK], BF16) for k in pieces}
         x8_codes = {k: tile("x8_codes%d_%d" % k[:2], [P, k[2]], U32) for k in pieces}
@@ -54,12 +54,11 @@ def tile_mix_atom_fm_pl_none_kernel(
         y32 = [tile("y32_%d" % c, [P, PACK, N], F32) for c in range(CHUNKS)]
         y_bf = [tile("y_bf%d" % c, [P, N, PACK], BF16) for c in range(CHUNKS)]
         y_codes = tile("y_codes", [P, T], U32)
-        y_plane = tile("y_plane", [P, T], U8)
+        y_plane = tile("y_plane", [P, T // 4], U8)
         acc = {}
 
-        def load_w8(a):
-            rows = w8[a * KP : (a + 1) * KP, :]
-            nc.sync.dma_start(out=w8_raw[a][:], in_=rows.rearrange("(p j) n -> p j n", j=PACK))
+        def load_w8():
+            nc.sync.dma_start(out=w8_raw[:], in_=w8.rearrange("(a p j) n -> p a (j n)", a=PASSES, j=PACK))
 
         def load_x8(k):
             a, t0, width = k
@@ -80,10 +79,10 @@ def tile_mix_atom_fm_pl_none_kernel(
                 in_=src.rearrange("p j (c i) -> p c j i", i=4),
             )
 
-        def round_w8(a, copy, m0, m1):
+        def round_w8(a, copy):
             copy(
-                out=w8_bf[a][:, :, m0:m1, :].rearrange("p r m j -> p m r j"),
-                in_=w8_raw[a][:, :, PACK * m0 : PACK * m1].rearrange("p j (m r) -> p m r j", r=PACK),
+                out=w8_bf[a][:].rearrange("p r m j -> p m r j"),
+                in_=w8_raw[:, a, :].rearrange("p (j m r) -> p m r j", j=PACK, r=PACK),
             )
 
         def quantize(codes, plane, src):
@@ -92,11 +91,11 @@ def tile_mix_atom_fm_pl_none_kernel(
         def quantize_w8(a):
             quantize(w8_codes[a][:], w8_plane[a][:], w8_bf[a][:].rearrange("p r m j -> p (r m j)"))
 
-        def round_x8(k):
-            interleave(nc.vector.tensor_copy, x8_bf[k][:], x8_raw[k][:])
+        def round_x8(k, lo=0, hi=N):
+            interleave(nc.vector.tensor_copy, x8_bf[k][:, lo:hi, :], x8_raw[k][:, :, lo:hi])
 
-        def quantize_x8(k):
-            quantize(x8_codes[k][:], x8_plane[k][:], x8_bf[k][:].rearrange("p t j -> p (t j)"))
+        def quantize_x8(k, lo=0, hi=N):
+            quantize(x8_codes[k][:, lo:hi], x8_plane[k][:, lo:hi], x8_bf[k][:, lo:hi, :].rearrange("p t j -> p (t j)"))
 
         def fp4_passes(c, tiles=range(PACK)):
             for r in tiles:
@@ -113,18 +112,17 @@ def tile_mix_atom_fm_pl_none_kernel(
                         stop=False,
                     )
 
-        def fp8_passes(k, tiles=range(PACK)):
-            a, t0, width = k
-            c, col = divmod(t0, N)
+        def fp8_passes(k, tiles=range(PACK), lo=0, hi=N):
+            a, c = k[0], k[1] // N
             for r in tiles:
                 nc.tensor.matmul_mx(
-                    out=acc[c, r][:, col : col + width],
+                    out=acc[c, r][:, lo:hi],
                     lhsT=w8_codes[a][:, P * r : P * (r + 1)].bitcast(FP8X4),
                     lhsT_scale=w8_plane[a][:, P * r : P * (r + 1)],
-                    rhs=x8_codes[k][:].bitcast(FP8X4),
-                    rhs_scale=x8_plane[k][:],
+                    rhs=x8_codes[k][:, lo:hi].bitcast(FP8X4),
+                    rhs_scale=x8_plane[k][:, lo:hi],
                     start=False,
-                    stop=(a == PASSES - 1 and col + width == N),
+                    stop=(a == PASSES - 1 and hi == N),
                 )
 
         def drain(c, r, copy):
@@ -134,8 +132,16 @@ def tile_mix_atom_fm_pl_none_kernel(
             interleave(copy, y_bf[c][:, lo:hi, :], y32[c][:, :, lo:hi])
 
         def quantize_y(c, lo=0, hi=N):
-            cols = slice(c * N + lo, c * N + hi)
-            quantize(y_codes[:, cols], y_plane[:, cols], y_bf[c][:, lo:hi, :].rearrange("p t j -> p (t j)"))
+            quarter = T // 4
+            while lo < hi:
+                u, col = divmod(c * N + lo, quarter)
+                end = min(hi, lo + quarter - col)
+                quantize(
+                    y_codes[:, c * N + lo : c * N + end],
+                    y_plane[4 * u :, col : col + end - lo],
+                    y_bf[c][:, lo:end, :].rearrange("p t j -> p (t j)"),
+                )
+                lo = end
 
         def store_y(c, r0, r1):
             rows = out_0.rearrange("(p r) t -> p r t", r=PACK)
@@ -154,16 +160,14 @@ def tile_mix_atom_fm_pl_none_kernel(
         load_words(x4_early, x4_words[:, :, : 4 * N])
         load_plane(w4_plane_raw, w4_scales)
         load_words(w4_raw, w4_words)
-        load_w8(0)
+        load_w8()
         load_plane(x4_plane, x4_scales)
-        load_w8(1)
         for k in sorted(pieces, key=lambda k: (k[1] // N, k[0], k[1])):
             if k == (0, 2 * N, N):
                 load_words(x4_late, x4_words[:, :, 4 * N :])
             load_x8(k)
 
-        round_w8(0, nc.scalar.copy, 0, P)
-        round_w8(1, nc.scalar.copy, 0, P // 2)
+        round_w8(1, nc.scalar.copy)
         nc.vector.tensor_copy(
             out=w4_plane[:].rearrange("p a (r m) -> p a r m", r=PACK),
             in_=w4_plane_raw[:].rearrange("p a (m r) -> p a r m", r=PACK),
@@ -174,20 +178,23 @@ def tile_mix_atom_fm_pl_none_kernel(
                 in_=w4_raw[:, a, :].rearrange("p (m r b) -> p r m b", r=PACK, b=2),
             )
         vcopy, scopy = nc.vector.tensor_copy, nc.scalar.copy
+        round_w8(0, vcopy)
         quantize_w8(0)
-        round_w8(1, vcopy, P // 2, P)
-        quantize_w8(1)
 
         def prepare_x8(k):
             round_x8(k)
             quantize_x8(k)
 
         last = CHUNKS - 1
-        halves = pieces[-2:]
+        halves = [(0, H), (H, N)]
 
         fp4_passes(0)
-        fp4_passes(1)
-        prepare_x8((0, 0, N))
+        fp4_passes(1, (0, 1))
+        k = (0, 0, N)
+        interleave(scopy, x8_bf[k][:, 384:, :], x8_raw[k][:, :, 384:])
+        interleave(vcopy, x8_bf[k][:, :384, :], x8_raw[k][:, :, :384])
+        quantize_w8(1)
+        quantize_x8((0, 0, N))
         fp8_passes((0, 0, N))
         k = (1, 0, N)
         interleave(scopy, x8_bf[k][:, SPLIT:, :], x8_raw[k][:, :, SPLIT:])
@@ -200,6 +207,7 @@ def tile_mix_atom_fm_pl_none_kernel(
         round_y(0, scopy, H, N)
         store_y(0, 0, 4)
 
+        fp4_passes(1, (2, 3))
         prepare_x8((0, N, N))
         fp8_passes((0, N, N))
         fp4_passes(last, (0, 1))
@@ -215,18 +223,18 @@ def tile_mix_atom_fm_pl_none_kernel(
         fp4_passes(last, (2, 3))
         round_x8((0, 2 * N, N))
         quantize_y(0, H, N)
-        store_codes(0, N)
         quantize_x8((0, 2 * N, N))
         fp8_passes((0, 2 * N, N))
-        for k in halves:
-            round_x8(k)
-        for k in halves:
-            quantize_x8(k)
+        for lo, hi in halves:
+            round_x8(pieces[-1], lo, hi)
+        for lo, hi in halves:
+            quantize_x8(pieces[-1], lo, hi)
         for u in range(2):
-            for k in halves:
-                fp8_passes(k, (2 * u, 2 * u + 1))
-        round_y(1, vcopy, 384, N)
+            for lo, hi in halves:
+                fp8_passes(pieces[-1], (2 * u, 2 * u + 1), lo, hi)
         quantize_y(1, 0, H)
+        store_codes(0, N + H)
+        round_y(1, vcopy, 384, N)
         for r in range(PACK):
             drain(last, r, scopy if r % 2 else vcopy)
         store_y(last, 0, 2)
@@ -235,9 +243,8 @@ def tile_mix_atom_fm_pl_none_kernel(
         round_y(last, vcopy, 0, H)
         quantize_y(1, H, N)
         quantize_y(last, 0, H)
-        store_codes(N, T - H)
         quantize_y(last, H, N)
-        store_codes(T - H, T)
-        scale_rows = out_2.rearrange("a (q s) t -> s q (a t)", s=4)
-        for s in range(4):
-            nc.scalar.dma_start(out=scale_rows[s].bitcast(I32), in_=y_plane[s:P:32, :].bitcast(I32))
+        store_codes(N + H, T)
+        scale_rows = out_2.rearrange("a (q s) (u t) -> (a q) u s t", s=4, u=4)
+        for q in range(4):
+            nc.scalar.dma_start(out=scale_rows[q].bitcast(I32), in_=y_plane[32 * q : 32 * q + 16, :].bitcast(I32))

@@ -68,10 +68,10 @@ def tile_mix_atom_fm_pl_none_kernel(
         def load_words(dst, words):
             nc.sync.dma_start(out=dst[:].bitcast(I32), in_=words.rearrange("a p b -> p a b").bitcast(I32))
 
-        def load_plane(plane, scales):
+        def load_plane(queue, plane, scales, which):
             rows = scales.rearrange("a (q s) n -> s q a n", s=4)
-            for s in range(4):
-                nc.sync.dma_start(out=plane[s:P:32, :, :].bitcast(I32), in_=rows[s].bitcast(I32))
+            for s in which:
+                queue.dma_start(out=plane[s:P:32, :, :].bitcast(I32), in_=rows[s].bitcast(I32))
 
         def interleave(copy, dst, src):
             copy(
@@ -158,10 +158,11 @@ def tile_mix_atom_fm_pl_none_kernel(
         nc.vector.memset(x4_plane[:].rearrange("p a n -> p (a n)").bitcast(I32), 0)
 
         load_words(x4_early, x4_words[:, :, : 4 * N])
-        load_plane(w4_plane_raw, w4_scales)
         load_words(w4_raw, w4_words)
+        load_plane(nc.scalar, w4_plane_raw, w4_scales, range(4))
+        load_plane(nc.sync, x4_plane, x4_scales, (0,))
         load_w8()
-        load_plane(x4_plane, x4_scales)
+        load_plane(nc.sync, x4_plane, x4_scales, (1, 2, 3))
         for k in sorted(pieces, key=lambda k: (k[1] // N, k[0], k[1])):
             if k == (0, 2 * N, N):
                 load_words(x4_late, x4_words[:, :, 4 * N :])

@@ -155,29 +155,27 @@ def tile_mix_atom_fm_pl_none_kernel(
             )
 
         nc.vector.memset(w4_plane_raw[:].rearrange("p a n -> p (a n)").bitcast(I32), 0)
-        nc.vector.memset(x4_plane[:].rearrange("p a n -> p (a n)").bitcast(I32), 0)
 
-        load_words(x4_early, x4_words[:, :, : 4 * N])
+        load_plane(nc.sync, x4_plane, x4_scales, range(4))
         load_words(w4_raw, w4_words)
-        load_plane(nc.scalar, w4_plane_raw, w4_scales, range(4))
-        load_plane(nc.sync, x4_plane, x4_scales, (0,))
         load_w8()
-        load_plane(nc.sync, x4_plane, x4_scales, (1, 2, 3))
+        load_plane(nc.sync, w4_plane_raw, w4_scales, range(4))
+        load_words(x4_early, x4_words[:, :, : 4 * N])
         for k in sorted(pieces, key=lambda k: (k[1] // N, k[0], k[1])):
             if k == (0, 2 * N, N):
                 load_words(x4_late, x4_words[:, :, 4 * N :])
             load_x8(k)
 
         round_w8(1, nc.scalar.copy)
-        nc.vector.tensor_copy(
-            out=w4_plane[:].rearrange("p a (r m) -> p a r m", r=PACK),
-            in_=w4_plane_raw[:].rearrange("p a (m r) -> p a r m", r=PACK),
-        )
         for a in range(PASSES):
             nc.vector.tensor_copy(
                 out=w4_dealt[:, a, :].rearrange("p (r m b) -> p r m b", r=PACK, b=2),
                 in_=w4_raw[:, a, :].rearrange("p (m r b) -> p r m b", r=PACK, b=2),
             )
+        nc.vector.tensor_copy(
+            out=w4_plane[:].rearrange("p a (r m) -> p a r m", r=PACK),
+            in_=w4_plane_raw[:].rearrange("p a (m r) -> p a r m", r=PACK),
+        )
         vcopy, scopy = nc.vector.tensor_copy, nc.scalar.copy
         round_w8(0, vcopy)
         quantize_w8(0)

@@ -156,7 +156,8 @@ def tile_mix_atom_fm_pl_none_kernel(
 
         nc.vector.memset(w4_plane_raw[:].rearrange("p a n -> p (a n)").bitcast(I32), 0)
 
-        load_plane(nc.sync, x4_plane, x4_scales, range(4))
+        load_plane(nc.sync, x4_plane, x4_scales, (0, 1))
+        load_plane(nc.scalar, x4_plane, x4_scales, (2, 3))
         load_words(w4_raw, w4_words)
         load_w8()
         load_plane(nc.sync, w4_plane_raw, w4_scales, range(4))

from contextlib import ExitStack

import concourse.mybir as mybir

O, K4, M, T = 1024, 1024, 512, 1536
FLOPS = 2 * (O + K4) * M * T

F32 = mybir.dt.float32
BF16 = mybir.dt.bfloat16
I32 = mybir.dt.int32
U32 = mybir.dt.uint32
U8 = mybir.dt.uint8
FP8X4 = mybir.dt.float8_e4m3fn_x4
FP4X4 = mybir.dt.float4_e2m1fn_x4

P = 128
PACK = 4
KP = P * PACK
PASSES = 2
N = 512
H = N // 2
CHUNKS = T // N
SPLIT = 320


def tile_mix_atom_fm_pl_none_kernel(
    tc, x8, w8, x4_words, x4_scales, w4_words, w4_scales, out_0, out_1, out_2
):
    nc = tc.nc
    with ExitStack() as ctx:
        sb = ctx.enter_context(tc.tile_pool(name="sb", bufs=1))
        psum = ctx.enter_context(tc.psum_pool(name="psum", bufs=1))
        ctx.enter_context(tc.manual_schedule())

        def tile(name, shape, dtype):
            return sb.tile(shape, dtype, name=name, align_bytes=256)

        w8_raw = tile("w8_raw", [P, PASSES, PACK * M], F32)
        w8_bf = [tile("w8_bf%d" % a, [P, PACK, P, PACK], BF16) for a in range(PASSES)]
        w8_codes = [tile("w8_codes%d" % a, [P, M], U32) for a in range(PASSES)]
        w8_plane = [tile("w8_plane%d" % a, [P, M], U8) for a in range(PASSES)]
        pieces = [(a, t0, N) for t0 in range(0, T, N) for a in range(PASSES)]
        x8_raw = {k: tile("x8_raw%d_%d" % k[:2], [P, PACK, k[2]], F32) for k in pieces}
        x8_bf = {k: tile("x8_bf%d_%d" % k[:2], [P, k[2], PACK], BF16) for k in pieces}
        x8_codes = {k: tile("x8_codes%d_%d" % k[:2], [P, k[2]], U32) for k in pieces}
        x8_plane = {k: tile("x8_plane%d_%d" % k[:2], [P, k[2]], U8) for k in pieces}
        w4_raw = tile("w4_raw", [P, PASSES, 2 * M], U8)
        w4_dealt = tile("w4_dealt", [P, PASSES, 2 * M], U8)
        w4_plane_raw = tile("w4_plane_raw", [P, PASSES, M], U8)
        w4_plane = tile("w4_plane", [P, PASSES, M], U8)
        x4_early = tile("x4_early", [P, PASSES, 4 * N], U8)
        x4_late = tile("x4_late", [P, PASSES, 2 * N], U8)
        x4_plane = tile("x4_plane", [P, PASSES, T], U8)
        y32 = [tile("y32_%d" % c, [P, PACK, N], F32) for c in range(CHUNKS)]
        y_bf = [tile("y_bf%d" % c, [P, N, PACK], BF16) for c in range(CHUNKS)]
        y_codes = tile("y_codes", [P, T], U32)
        y_plane = tile("y_plane", [P, T // 4], U8)
        acc = {}

        def load_w8():
            nc.sync.dma_start(out=w8_raw[:], in_=w8.rearrange("(a p j) n -> p a (j n)", a=PASSES, j=PACK))

        def load_x8(k):
            a, t0, width = k
            rows = x8[a * KP : (a + 1) * KP, t0 : t0 + width]
            nc.sync.dma_start(out=x8_raw[k][:], in_=rows.rearrange("(p j) t -> p j t", j=PACK))

        def load_words(dst, words):
            nc.sync.dma_start(out=dst[:].bitcast(I32), in_=words.rearrange("a p b -> p a b").bitcast(I32))

        def load_plane(queue, plane, scales, which):
            rows = scales.rearrange("a (q s) n -> s q a n", s=4)
            for s in which:
                queue.dma_start(out=plane[s:P:32, :, :].bitcast(I32), in_=rows[s].bitcast(I32))

        def interleave(copy, dst, src):
            copy(
                out=dst.rearrange("p (c i) j -> p c j i", i=4),
                in_=src.rearrange("p j (c i) -> p c j i", i=4),
            )

        def round_w8(a, copy):
            copy(
                out=w8_bf[a][:].rearrange("p r m j -> p m r j"),
                in_=w8_raw[:, a, :].rearrange("p (j m r) -> p m r j", j=PACK, r=PACK),
            )

        def quantize(codes, plane, src):
            nc.vector.quantize_mx(out=codes.bitcast(FP8X4), scales=plane, in_=src)

        def quantize_w8(a):
            quantize(w8_codes[a][:], w8_plane[a][:], w8_bf[a][:].rearrange("p r m j -> p (r m j)"))

        def round_x8(k, lo=0, hi=N):
            interleave(nc.vector.tensor_copy, x8_bf[k][:, lo:hi, :], x8_raw[k][:, :, lo:hi])

        def quantize_x8(k, lo=0, hi=N):
            quantize(x8_codes[k][:, lo:hi], x8_plane[k][:, lo:hi], x8_bf[k][:, lo:hi, :].rearrange("p t j -> p (t j)"))

        def fp4_passes(c, tiles=range(PACK)):
            for r in tiles:
                name = "acc%d_%d" % (c % 2, r)
                acc[c, r] = psum.tile([P, N], F32, name=name)
                for a in range(PASSES):
                    nc.tensor.matmul_mx(
                        out=acc[c, r][:],
                        lhsT=w4_dealt[:, a, 2 * P * r : 2 * P * (r + 1)].bitcast(FP4X4),
                        lhsT_scale=w4_plane[:, a, P * r : P * (r + 1)],
                        rhs=(x4_late[:, a, :] if c == CHUNKS - 1 else x4_early[:, a, 2 * N * c : 2 * N * (c + 1)]).bitcast(FP4X4),
                        rhs_scale=x4_plane[:, a, N * c : N * (c + 1)],
                        start=(a == 0),
                        stop=False,
                    )

        def fp8_passes(k, tiles=range(PACK), lo=0, hi=N):
            a, c = k[0], k[1] // N
            for r in tiles:
                nc.tensor.matmul_mx(
                    out=acc[c, r][:, lo:hi],
                    lhsT=w8_codes[a][:, P * r : P * (r + 1)].bitcast(FP8X4),
                    lhsT_scale=w8_plane[a][:, P * r : P * (r + 1)],
                    rhs=x8_codes[k][:, lo:hi].bitcast(FP8X4),
                    rhs_scale=x8_plane[k][:, lo:hi],
                    start=False,
                    stop=(a == PASSES - 1 and hi == N),
                )

        def drain(c, r, copy):
            copy(out=y32[c][:, r, :], in_=acc[c, r][:])

        def round_y(c, copy, lo, hi):
            interleave(copy, y_bf[c][:, lo:hi, :], y32[c][:, :, lo:hi])

        def quantize_y(c, lo=0, hi=N):
            quarter = T // 4
            while lo < hi:
                u, col = divmod(c * N + lo, quarter)
                end = min(hi, lo + quarter - col)
                quantize(
                    y_codes[:, c * N + lo : c * N + end],
                    y_plane[4 * u :, col : col + end - lo],
                    y_bf[c][:, lo:end, :].rearrange("p t j -> p (t j)"),
                )
                lo = end

        def store_y(c, r0, r1):
            rows = out_0.rearrange("(p r) t -> p r t", r=PACK)
            nc.sync.dma_start(out=rows[:, r0:r1, c * N : (c + 1) * N], in_=y32[c][:, r0:r1, :])

        def store_codes(t0, t1):
            cols = slice(t0, t1)
            nc.sync.dma_start(
                out=out_1.rearrange("a p t i -> p (a t i)").bitcast(I32)[:, cols],
                in_=y_codes[:, cols].bitcast(I32),
            )

        nc.vector.memset(w4_plane_raw[:].rearrange("p a n -> p (a n)").bitcast(I32), 0)

        load_plane(nc.sync, x4_plane, x4_scales, (0, 1))
        load_plane(nc.scalar, x4_plane, x4_scales, (2, 3))
        load_words(w4_raw, w4_words)
        load_w8()
        load_plane(nc.sync, w4_plane_raw, w4_scales, range(4))
        load_words(x4_early, x4_words[:, :, : 4 * N])
        for k in sorted(pieces, key=lambda k: (k[1] // N, k[0], k[1])):
            if k == (0, 2 * N, N):
                load_words(x4_late, x4_words[:, :, 4 * N :])
            load_x8(k)

        round_w8(1, nc.scalar.copy)
        for a in range(PASSES):
            nc.vector.tensor_copy(
                out=w4_dealt[:, a, :].rearrange("p (r m b) -> p r m b", r=PACK, b=2),
                in_=w4_raw[:, a, :].rearrange("p (m r b) -> p r m b", r=PACK, b=2),
            )
        nc.vector.tensor_copy(
            out=w4_plane[:].rearrange("p a (r m) -> p a r m", r=PACK),
            in_=w4_plane_raw[:].rearrange("p a (m r) -> p a r m", r=PACK),
        )
        vcopy, scopy = nc.vector.tensor_copy, nc.scalar.copy
        round_w8(0, vcopy)
        quantize_w8(0)

        def prepare_x8(k):
            round_x8(k)
            quantize_x8(k)

        last = CHUNKS - 1
        halves = [(0, H), (H, N)]

        fp4_passes(0)
        fp4_passes(1, (0, 1))
        k = (0, 0, N)
        interleave(scopy, x8_bf[k][:, 384:, :], x8_raw[k][:, :, 384:])
        interleave(vcopy, x8_bf[k][:, :384, :], x8_raw[k][:, :, :384])
        quantize_w8(1)
        quantize_x8((0, 0, N))
        fp8_passes((0, 0, N))
        k = (1, 0, N)
        interleave(scopy, x8_bf[k][:, SPLIT:, :], x8_raw[k][:, :, SPLIT:])
        interleave(vcopy, x8_bf[k][:, :SPLIT, :], x8_raw[k][:, :, :SPLIT])
        quantize_x8(k)
        fp8_passes(k)
        for r in range(PACK):
            drain(0, r, scopy)
        round_y(0, scopy, 0, H)
        round_y(0, scopy, H, N)
        store_y(0, 0, 4)

        fp4_passes(1, (2, 3))
        prepare_x8((0, N, N))
        fp8_passes((0, N, N))
        fp4_passes(last, (0, 1))
        prepare_x8((1, N, N))
        fp8_passes((1, N, N))
        for r in range(PACK):
            drain(1, r, scopy)
        quantize_y(0, 0, H)
        store_y(1, 0, 4)
        round_y(1, scopy, 0, H)
        round_y(1, scopy, H, 384)

        fp4_passes(last, (2, 3))
        round_x8((0, 2 * N, N))
        quantize_y(0, H, N)
        quantize_x8((0, 2 * N, N))
        fp8_passes((0, 2 * N, N))
        for lo, hi in halves:
            round_x8(pieces[-1], lo, hi)
        for lo, hi in halves:
            quantize_x8(pieces[-1], lo, hi)
        for u in range(2):
            for lo, hi in halves:
                fp8_passes(pieces[-1], (2 * u, 2 * u + 1), lo, hi)
        quantize_y(1, 0, H)
        store_codes(0, N + H)
        round_y(1, vcopy, 384, N)
        for r in range(PACK):
            drain(last, r, scopy if r % 2 else vcopy)
        store_y(last, 0, 2)
        store_y(last, 2, 4)
        round_y(last, scopy, H, N)
        round_y(last, vcopy, 0, H)
        quantize_y(1, H, N)
        quantize_y(last, 0, H)
        quantize_y(last, H, N)
        store_codes(N + H, T)
        scale_rows = out_2.rearrange("a (q s) (u t) -> (a q) u s t", s=4, u=4)
        for q in range(4):
            nc.scalar.dma_start(out=scale_rows[q].bitcast(I32), in_=y_plane[32 * q : 32 * q + 16, :].bitcast(I32))
